import numpy as np
import ml_dtypes


def mxq(x, axis, fmt="e4m3"):
    dtype, down = {"e4m3": (ml_dtypes.float8_e4m3fn, 7), "e5m2": (ml_dtypes.float8_e5m2, 14)}[fmt]
    v = np.moveaxis(np.asarray(x, np.float32).astype(ml_dtypes.bfloat16).astype(np.float64), axis, -1)
    blocks = v.reshape(v.shape[:-1] + (-1, 32))
    amax = np.abs(blocks).max(-1, keepdims=True)
    byte = np.maximum(np.where(amax > 0, np.frexp(amax)[1] - 1 + 127, 0) - down, 1)
    scale = np.exp2(byte - 127.0)
    codes = (blocks / scale).astype(np.float32).astype(dtype).astype(np.float64)
    return np.moveaxis((codes * scale).reshape(v.shape), -1, axis)


WIDE = False


def mx_kscale(k):
    if not WIDE:
        return np.ones(k)
    levels = np.array([10, -10, 5, -5, 0])
    if k % 512:
        return np.exp2(np.random.permutation(np.resize(levels, k // 32))).repeat(32)
    a = np.empty((k // 512, 16))
    for p in range(k // 512):
        a[p, :8] = np.random.permutation(np.resize(levels, 8))
        for g in range(8):
            far = levels[np.abs(levels - a[p, g]) >= 10]
            a[p, g + 8] = far[np.random.randint(len(far))]
    return np.exp2(a.ravel()).repeat(32)


def f64(x):
    return np.asarray(x).astype(np.float64)


def striped(idx):
    return np.tile(idx.reshape(-1, 16).T, (8, 1)).astype(np.uint16)


def unstriped(offs):
    return offs[:16].T.reshape(-1).astype(np.int64)


def pack_weight(w):
    k, n = w.shape
    w = f64(np.asarray(w, np.float32).astype(ml_dtypes.bfloat16)).reshape(k // 32, 32, n)
    amax = np.abs(w).max(1)
    byte = np.clip(np.where(amax > 0, np.frexp(amax)[1] - 1 + 127 - 7, 1), 1, 254)
    scaled = (w * np.exp2(127.0 - byte)[:, None, :]).reshape(k, n).astype(np.float32)
    words = np.ascontiguousarray(scaled.reshape(k // 512, 128, 4, n).transpose(0, 1, 3, 2)).astype(ml_dtypes.float8_e4m3fn).view(np.uint8)
    return words, np.ascontiguousarray(byte.astype(np.uint8).reshape(k // 512, 16, n))


def unpack_weight(words, scales):
    g, p, n, _ = words.shape
    vals = np.ascontiguousarray(words).view(ml_dtypes.float8_e4m3fn).astype(np.float64) * np.repeat(np.exp2(scales.astype(np.float64) - 127.0), 8, axis=1)[..., None]
    return vals.transpose(0, 1, 3, 2).reshape(g * 512, n)


def planes(y):
    n, m = y.shape
    v = y.astype(np.float32).astype(ml_dtypes.bfloat16).astype(np.float64).reshape(n // 32, 32, m)
    top = np.abs(v).max(1)
    byte = np.clip(np.where(top > 0, np.frexp(top)[1] - 1 + 127 - 7, 1), 1, 254)
    codes = (v * np.exp2(127.0 - byte)[:, None, :]).reshape(n, m).astype(np.float32).astype(ml_dtypes.float8_e4m3fn).view(np.uint8)
    words = codes.reshape(n // 512, 128, 4, m).transpose(0, 1, 3, 2)
    return np.ascontiguousarray(words), np.ascontiguousarray(byte.astype(np.uint8).reshape(n // 512, 16, m))


K, T, S, V, H, N = 512, 1024, 512, 256, 512, 512


def setup_inputs():
    n = np.random.standard_normal
    s = mx_kscale(K)[:, None]
    u = mx_kscale(H)
    near = np.random.permutation(S)
    packed_xT = pack_weight(n((K, T)) * s)
    return {
        "x_words": packed_xT[0],
        "x_scales": packed_xT[1],
        "w1": (n((K, N)) / np.sqrt(K) / s).astype(np.float32),
        "w2": (n((K, N)) / np.sqrt(K) / s).astype(np.float32),
        "w3": (n((K, H)) / np.sqrt(K) / s * u).astype(np.float32),
        "w4": (n((H, N)) / np.sqrt(H) / u[:, None]).astype(np.float32),
        "offs": striped(np.random.permutation(T)[:S]),
        "tgt": striped(np.random.permutation(T)[:V]),
        "pos1": striped(near[:V]),
        "pos2": striped(near[V:]),
        "pos3": striped(np.random.permutation(S)[:V]),
    }


def reference(x_words, x_scales, w1, w2, w3, w4, offs, tgt, pos1, pos2, pos3):
    xq = unpack_weight(x_words, x_scales)[:, unstriped(offs)]
    e = mxq(f64(w2), 0, "e4m3").T @ xq
    x_tgt = unpack_weight(x_words, x_scales)[:, unstriped(tgt)]
    y = mxq(f64(w1), 0, "e4m3").T @ x_tgt
    a0 = np.tanh(e[:, unstriped(pos1)] * y)
    h = mxq(f64(w3), 0, "e4m3").T @ xq
    a1 = np.tanh(e[:, unstriped(pos2)] * y)
    a2 = np.tanh(e[:, unstriped(pos3)] * y)
    z = a0 * h[:, unstriped(pos1)] + a1 * h[:, unstriped(pos2)] + a2 * h[:, unstriped(pos3)]
    out_0 = mxq(f64(w4), 0, "e4m3").T @ mxq(z, 0, "e4m3")
    return (out_0,) + planes(out_0)

@@ -1,0 +1,267 @@
+from contextlib import ExitStack
+
+import concourse.mybir as mybir
+from concourse.masks import make_identity
+
+F32 = mybir.dt.float32
+BF16 = mybir.dt.bfloat16
+I32 = mybir.dt.int32
+U32 = mybir.dt.uint32
+U16 = mybir.dt.uint16
+U8 = mybir.dt.uint8
+FP8X4 = mybir.dt.float8_e4m3fn_x4
+MULT = mybir.AluOpType.mult
+COPY = mybir.ActivationFunctionType.Copy
+TANH = mybir.ActivationFunctionType.Tanh
+
+P = 128
+PACK = 4
+K, T, S, V, H, N = 512, 1024, 512, 256, 512, 512
+D = 3
+PIECES = ((0, 128), (128, 128), (256, 256))
+FLOPS = 2 * K * (N * S + H * S + N * V) + 2 * H * N * V
+
+
+def tile_picked_zdin_tanh_po_kernel(
+    tc, x_words, x_scales, w1, w2, w3, w4, offs, tgt, pos1, pos2, pos3, out_0, out_1, out_2
+):
+    nc = tc.nc
+    with ExitStack() as ctx:
+        keep = ctx.enter_context(tc.tile_pool(name="keep", bufs=1))
+        psum = ctx.enter_context(tc.psum_pool(name="psum", bufs=1))
+
+        def load_list(src, name):
+            lst = keep.tile([P, src.shape[1]], U16, name=name)
+            nc.sync.dma_start(lst[:], src)
+            return lst
+
+        def load_weight(queue, w, c0, width, name):
+            raw = keep.tile([P, PACK, width], F32, name=name)
+            queue.dma_start(raw[:], w[:, c0 : c0 + width].rearrange("(p j) c -> p j c", j=PACK))
+            return raw
+
+        xs = keep.tile([P, T], U8, name="xs")
+        nc.gpsimd.memset(xs[:].bitcast(U32), 0)
+        for q in range(4):
+            queue = nc.scalar if q % 2 else nc.sync
+            queue.dma_start(
+                xs[32 * q : 32 * q + 4, :].bitcast(I32), x_scales[0, 4 * q : 4 * q + 4, :].bitcast(I32)
+            )
+        offs_sb = load_list(offs, "offs_sb")
+        xw = keep.tile([P, T], U32, name="xw")
+        nc.scalar.dma_start(xw[:].bitcast(I32), x_words[0].rearrange("p c r -> p (c r)").bitcast(I32))
+        tgt_sb = load_list(tgt, "tgt_sb")
+        raws = {}
+        for piece, (c0, width) in enumerate(PIECES):
+            for name, w in (("w2", w2), ("w1", w1), ("w3", w3)):
+                raws[name, piece] = load_weight(nc.sync, w, c0, width, "%s_raw%d" % (name, piece))
+            if piece == 0:
+                pos_sb = [load_list(src, "pos_sb%d" % d) for d, src in enumerate((pos1, pos2, pos3))]
+        w4_raw = load_weight(nc.sync, w4, 0, N, "w4_raw")
+
+        ident = keep.tile([P, P], F32, name="ident")
+        make_identity(nc, ident[:])
+
+        def copy_on(engine, out, in_):
+            if engine == "vector":
+                nc.vector.tensor_copy(out, in_)
+            else:
+                nc.scalar.copy(out, in_)
+
+        def pick(table, lst, n, dtype, name, tag=""):
+            picked = keep.tile([P, n], dtype, name=name, tag=tag or name, align_bytes=64)
+            nc.vector.tensor_copy(picked[:], table[:].indirect(lst[:]))
+            return picked
+
+        def round_weight(key, engine, tag=""):
+            name = "%s_bf%d" % key
+            grouped = keep.tile([P, raws[key].shape[2], PACK], BF16, name=name, tag=tag or name, align_bytes=64)
+            copy_on(
+                engine,
+                grouped[:].rearrange("p (c i) j -> p c j i", i=4),
+                raws[key][:].rearrange("p j (c i) -> p c j i", i=4),
+            )
+            return grouped[:].rearrange("p c j -> p (c j)")
+
+        def quantize(values, name):
+            n = values.shape[1] // PACK
+            words = keep.tile([P, n], U32, name=name + "_words", align_bytes=64)
+            scales = keep.tile([P, n], U8, name=name + "_scales", align_bytes=64)
+            nc.vector.quantize_mx(out=words[:].bitcast(FP8X4), scales=scales[:], in_=values)
+            return words, scales
+
+        def product(out, weights, cols, moving):
+            nc.tensor.matmul_mx(
+                out=out,
+                lhsT=weights[0][:, cols].bitcast(FP8X4),
+                lhsT_scale=weights[1][:, cols],
+                rhs=moving[0][:].bitcast(FP8X4),
+                rhs_scale=moving[1][:],
+                start=True,
+                stop=True,
+            )
+
+        def product_rows(weights, a, moving, bank, name):
+            rows = psum.tile([P, moving[0].shape[1]], F32, name=name + "_ps", tag="bank%d" % bank)
+            product(rows[:], weights, slice(a * P, (a + 1) * P), moving)
+            return rows
+
+        def to_sbuf(rows, name):
+            held = keep.tile(rows.shape, F32, name=name, align_bytes=64)
+            nc.scalar.copy(held[:], rows[:])
+            return held
+
+        def scores(e, y, name):
+            pre = keep.tile([P, D, V], F32, name=name)
+            for d in range(D):
+                nc.vector.tensor_tensor(pre[:, d, :], e[:].indirect(pos_sb[d][:]), y[:], MULT)
+            return pre
+
+        def fetch(h, v0, n, name):
+            got = keep.tile([P, D, n], F32, name=name, align_bytes=64)
+            for d in range(D):
+                nc.scalar.activation(
+                    got[:, d, :], h[:].indirect(pos_sb[d][:, v0 // 16 : (v0 + n) // 16]), COPY
+                )
+            return got
+
+        def squash(pre, name):
+            att = keep.tile([P, D, V], F32, name=name)
+            nc.scalar.activation(att[:].rearrange("p d v -> p (d v)"), pre[:].rearrange("p d v -> p (d v)"), TANH)
+            return att
+
+        def weigh(h, att, v0, n, name):
+            terms = keep.tile([P, D, n], F32, name=name)
+            for d in range(D):
+                nc.vector.tensor_tensor(
+                    terms[:, d, :],
+                    h[:].indirect(pos_sb[d][:, v0 // 16 : (v0 + n) // 16]),
+                    att[:, d, v0 : v0 + n],
+                    MULT,
+                )
+            return terms
+
+        def add_turned(terms, c0, out):
+            for d in range(D):
+                nc.tensor.matmul(
+                    out,
+                    lhsT=terms[:, d, c0 : c0 + P],
+                    rhs=ident[:],
+                    is_transpose=True,
+                    start=(d == 0),
+                    stop=(d == D - 1),
+                )
+
+        def round_z(g, t0, turned):
+            nc.scalar.copy(
+                z_bf[g][:, :, 32 * t0 : 32 * t0 + turned.shape[1] // PACK, :],
+                turned[:].rearrange("v (p u e) -> v u p e", u=2, e=2),
+            )
+
+        hist_scales = pick(xs, offs_sb, S, U8, "hist_scales")
+        tgt_scales = pick(xs, tgt_sb, V, U8, "tgt_scales")
+        hist = pick(xw, offs_sb, S, U32, "hist_words"), hist_scales
+        w2a = quantize(round_weight(("w2", 0), "scalar"), "w2a")
+        w1a = quantize(round_weight(("w1", 0), "scalar"), "w1a")
+        targets = pick(xw, tgt_sb, V, U32, "tgt_words", "w2_bf0"), tgt_scales
+        bf3 = round_weight(("w3", 0), "scalar")
+        e0 = to_sbuf(product_rows(w2a, 0, hist, 0, "e0"), "e0")
+        y0 = to_sbuf(product_rows(w1a, 0, targets, 1, "y0"), "y0")
+        w3a = quantize(bf3, "w3a")
+        bf2 = round_weight(("w2", 1), "vector", "w1_bf0")
+        bf1 = round_weight(("w1", 1), "vector")
+        w2b = quantize(bf2, "w2b")
+        w1b = quantize(bf1, "w1b")
+        s0 = scores(e0, y0, "s0")
+        bf3 = round_weight(("w3", 1), "scalar")
+        h0 = to_sbuf(product_rows(w3a, 0, hist, 2, "h0"), "h0")
+        w3b = quantize(bf3, "w3b")
+        e1 = to_sbuf(product_rows(w2b, 0, hist, 3, "e1"), "e1")
+        y1 = to_sbuf(product_rows(w1b, 0, targets, 4, "y1"), "y1")
+        s1 = scores(e1, y1, "s1")
+        w2c = quantize(round_weight(("w2", 2), "scalar"), "w2c")
+        a0 = squash(s0, "a0")
+        terms0 = weigh(h0, a0, 0, V, "terms0")
+        w1c = quantize(round_weight(("w1", 2), "scalar"), "w1c")
+        a1 = squash(s1, "a1")
+        h1 = to_sbuf(product_rows(w3b, 0, hist, 5, "h1"), "h1")
+        terms1 = weigh(h1, a1, 0, V, "terms1")
+        w3c = quantize(round_weight(("w3", 2), "scalar"), "w3c")
+        e2 = to_sbuf(product_rows(w2c, 0, hist, 6, "e2"), "e2")
+        y2 = to_sbuf(product_rows(w1c, 0, targets, 7, "y2"), "y2")
+        s2 = scores(e2, y2, "s2")
+        e3 = to_sbuf(product_rows(w2c, 1, hist, 0, "e3"), "e3")
+        y3 = to_sbuf(product_rows(w1c, 1, targets, 1, "y3"), "y3")
+        s3 = scores(e3, y3, "s3")
+        h2 = to_sbuf(product_rows(w3c, 0, hist, 2, "h2"), "h2")
+        h3 = to_sbuf(product_rows(w3c, 1, hist, 3, "h3"), "h3")
+        a2 = squash(s2, "a2")
+        terms2 = weigh(h2, a2, 0, V, "terms2")
+        values3 = [fetch(h3, g * P, P, "values3_%d" % g) for g in range(2)]
+        a3 = keep.tile([P, 2, D, P], F32, name="a3", tag="h3", align_bytes=64)
+        last = []
+        for g in range(2):
+            nc.scalar.activation(a3[:, g], s3[:, :, g * P : (g + 1) * P], TANH)
+            terms = keep.tile([P, D, P], F32, name="terms3_%d" % g)
+            nc.vector.tensor_tensor(terms[:], values3[g][:], a3[:, g], MULT)
+            last.append(terms)
+
+        z_t = [psum.tile([P, 3 * P], F32, name="z_t%d" % g, tag="bank%d" % (2 + g)) for g in range(2)]
+        z_bf = [keep.tile([P, 2, P, 2], BF16, name="z_bf%d" % g) for g in range(2)]
+        for t, terms in enumerate((terms0, terms1, terms2)):
+            for g in range(2):
+                add_turned(terms, g * P, z_t[g][:, t * P : (t + 1) * P])
+        for g in range(2):
+            round_z(g, 0, z_t[g])
+        w4_bf = []
+        for half in range(2):
+            dealt = keep.tile([P, 2, P, PACK], BF16, name="w4_bf%d" % half, align_bytes=64, tag="values3_%d" % half)
+            nc.vector.tensor_copy(
+                dealt[:].rearrange("p t m j -> p m t j"),
+                w4_raw[:].rearrange("p j (m t) -> p m t j", t=PACK)[:, :, 2 * half : 2 * half + 2, :],
+            )
+            w4_bf.append(dealt)
+        w4q = [quantize(w4_bf[half][:].rearrange("p t m j -> p (t m j)"), "w4q%d" % half) for half in range(2)]
+
+        out_words = keep.tile([P, V], U32, name="out_words", align_bytes=64)
+        out_scales = keep.tile([P, V], U8, name="out_scales", align_bytes=64)
+        out_rows = out_0.rearrange("(p t) v -> p t v", t=PACK)
+        word_rows = out_1[0].rearrange("p c r -> p (c r)").bitcast(I32)
+        zq = []
+        for g in range(2):
+            z_last = psum.tile([P, P], F32, name="z_last%d" % g, tag="bank%d" % g)
+            add_turned(last[g], 0, z_last[:])
+            round_z(g, 3, z_last)
+        for g in range(2):
+            back = psum.tile([P, 2, P], F32, name="back%d" % g, tag="bank%d" % (4 + g))
+            pairs = z_bf[g][:].rearrange("v u p e -> v (u p e)").bitcast(F32)
+            for u in range(2):
+                nc.tensor.transpose(back[:, u, :], pairs[:, u * P : (u + 1) * P], ident[:])
+            z_k = keep.tile([P, P * PACK], BF16, name="z_k%d" % g, align_bytes=64)
+            nc.scalar.copy(
+                z_k[:].bitcast(F32).rearrange("p (v u) -> p v u", u=2), back[:].rearrange("p u v -> p v u")
+            )
+            zq.append(quantize(z_k[:], "zq%d" % g))
+        for g in range(2):
+            cols = slice(g * P, (g + 1) * P)
+            res = psum.tile([P, PACK, P], F32, name="res%d" % g, tag="bank%d" % (6 + g))
+            for t in range(PACK):
+                product(res[:, t, :], w4q[t // 2], slice(t % 2 * P, (t % 2 + 1) * P), zq[g])
+            res_sb = keep.tile([P, PACK, P], F32, name="res_sb%d" % g)
+            nc.scalar.copy(res_sb[:], res[:])
+            nc.sync.dma_start(out_rows[:, :, cols], res_sb[:])
+            res_bf = keep.tile([P, P, PACK], BF16, name="res_bf%d" % g, align_bytes=64)
+            nc.vector.tensor_copy(
+                res_bf[:].rearrange("p (c i) t -> p c t i", i=4), res_sb[:].rearrange("p t (c i) -> p c t i", i=4)
+            )
+            nc.vector.quantize_mx(
+                out=out_words[:, cols].bitcast(FP8X4),
+                scales=out_scales[:, cols],
+                in_=res_bf[:].rearrange("p c t -> p (c t)"),
+            )
+            nc.sync.dma_start(word_rows[:, cols], out_words[:, cols].bitcast(I32))
+        for q in range(4):
+            queue = nc.scalar if q % 2 else nc.sync
+            queue.dma_start(
+                out_2[0, 4 * q : 4 * q + 4, :].bitcast(I32), out_scales[32 * q : 32 * q + 4, :].bitcast(I32)
+            )

@@ -179,7 +179,7 @@ def tile_picked_zdin_tanh_po_kernel(
         e1 = to_sbuf(product_rows(w2b, 0, hist, 3, "e1"), "e1")
         y1 = to_sbuf(product_rows(w1b, 0, targets, 4, "y1"), "y1")
         s1 = scores(e1, y1, "s1")
-        w2c = quantize(round_weight(("w2", 2), "scalar"), "w2c")
+        w2c = quantize(round_weight(("w2", 2), "vector"), "w2c")
         a0 = squash(s0, "a0")
         terms0 = weigh(h0, a0, 0, V, "terms0")
         w1c = quantize(round_weight(("w1", 2), "scalar"), "w1c")
@@ -197,14 +197,10 @@ def tile_picked_zdin_tanh_po_kernel(
         h3 = to_sbuf(product_rows(w3c, 1, hist, 3, "h3"), "h3")
         a2 = squash(s2, "a2")
         terms2 = weigh(h2, a2, 0, V, "terms2")
-        values3 = [fetch(h3, g * P, P, "values3_%d" % g) for g in range(2)]
-        a3 = keep.tile([P, 2, D, P], F32, name="a3", tag="h3", align_bytes=64)
-        last = []
-        for g in range(2):
-            nc.scalar.activation(a3[:, g], s3[:, :, g * P : (g + 1) * P], TANH)
-            terms = keep.tile([P, D, P], F32, name="terms3_%d" % g)
-            nc.vector.tensor_tensor(terms[:], values3[g][:], a3[:, g], MULT)
-            last.append(terms)
+        a3 = squash(s3, "a3")
+        values3 = fetch(h3, P, P, "values3")
+        last = [weigh(h3, a3, 0, P, "terms3_0"), keep.tile([P, D, P], F32, name="terms3_1")]
+        nc.vector.tensor_tensor(last[1][:], values3[:], a3[:, :, P:], MULT)
 
         z_t = [psum.tile([P, 3 * P], F32, name="z_t%d" % g, tag="bank%d" % (2 + g)) for g in range(2)]
         z_bf = [keep.tile([P, 2, P, 2], BF16, name="z_bf%d" % g) for g in range(2)]
@@ -215,10 +211,10 @@ def tile_picked_zdin_tanh_po_kernel(
             round_z(g, 0, z_t[g])
         w4_bf = []
         for half in range(2):
-            dealt = keep.tile([P, 2, P, PACK], BF16, name="w4_bf%d" % half, align_bytes=64, tag="values3_%d" % half)
+            dealt = keep.tile([P, 2, P, PACK], BF16, name="w4_bf%d" % half, align_bytes=64, tag=("h3", "values3")[half])
             nc.vector.tensor_copy(
-                dealt[:].rearrange("p t m j -> p m t j"),
-                w4_raw[:].rearrange("p j (m t) -> p m t j", t=PACK)[:, :, 2 * half : 2 * half + 2, :],
+                dealt[:].rearrange("p t m j -> p m j t"),
+                w4_raw[:].rearrange("p j (m t) -> p m j t", t=PACK)[:, :, :, 2 * half : 2 * half + 2],
             )
             w4_bf.append(dealt)
         w4q = [quantize(w4_bf[half][:].rearrange("p t m j -> p (t m j)"), "w4q%d" % half) for half in range(2)]

@@ -16,9 +16,12 @@ TANH = mybir.ActivationFunctionType.Tanh
 
 P = 128
 PACK = 4
+QUADRANTS = 4
+GROUPS = 2
+LINE = 4
 K, T, S, V, H, N = 512, 1024, 512, 256, 512, 512
 D = 3
-PIECES = ((0, 128), (128, 128), (256, 256))
+PIECES = ((0, P), (P, P), (2 * P, 2 * P))
 FLOPS = 2 * K * (N * S + H * S + N * V) + 2 * H * N * V
 
 
@@ -35,14 +38,14 @@ def tile_picked_zdin_tanh_po_kernel(
             nc.sync.dma_start(lst[:], src)
             return lst
 
-        def load_weight(queue, w, c0, width, name):
+        def load_weight(w, c0, width, name):
             raw = keep.tile([P, PACK, width], F32, name=name)
-            queue.dma_start(raw[:], w[:, c0 : c0 + width].rearrange("(p j) c -> p j c", j=PACK))
+            nc.sync.dma_start(raw[:], w[:, c0 : c0 + width].rearrange("(p j) c -> p j c", j=PACK))
             return raw
 
         xs = keep.tile([P, T], U8, name="xs")
         nc.gpsimd.memset(xs[:].bitcast(U32), 0)
-        for q in range(4):
+        for q in range(QUADRANTS):
             queue = nc.scalar if q % 2 else nc.sync
             queue.dma_start(
                 xs[32 * q : 32 * q + 4, :].bitcast(I32), x_scales[0, 4 * q : 4 * q + 4, :].bitcast(I32)
@@ -54,10 +57,10 @@ def tile_picked_zdin_tanh_po_kernel(
         raws = {}
         for piece, (c0, width) in enumerate(PIECES):
             for name, w in (("w2", w2), ("w1", w1), ("w3", w3)):
-                raws[name, piece] = load_weight(nc.sync, w, c0, width, "%s_raw%d" % (name, piece))
+                raws[name, piece] = load_weight(w, c0, width, "%s_raw%d" % (name, piece))
             if piece == 0:
                 pos_sb = [load_list(src, "pos_sb%d" % d) for d, src in enumerate((pos1, pos2, pos3))]
-        w4_raw = load_weight(nc.sync, w4, 0, N, "w4_raw")
+        w4_raw = load_weight(w4, 0, N, "w4_raw")
 
         ident = keep.tile([P, P], F32, name="ident")
         make_identity(nc, ident[:])
@@ -73,13 +76,14 @@ def tile_picked_zdin_tanh_po_kernel(
             nc.vector.tensor_copy(picked[:], table[:].indirect(lst[:]))
             return picked
 
-        def round_weight(key, engine, tag=""):
-            name = "%s_bf%d" % key
-            grouped = keep.tile([P, raws[key].shape[2], PACK], BF16, name=name, tag=tag or name, align_bytes=64)
+        def round_weight(name, piece, engine, tag=""):
+            raw = raws[name, piece]
+            tile_name = "%s_bf%d" % (name, piece)
+            grouped = keep.tile([P, raw.shape[2], PACK], BF16, name=tile_name, tag=tag or tile_name, align_bytes=64)
             copy_on(
                 engine,
-                grouped[:].rearrange("p (c i) j -> p c j i", i=4),
-                raws[key][:].rearrange("p j (c i) -> p c j i", i=4),
+                grouped[:].rearrange("p (c i) j -> p c j i", i=LINE),
+                raw[:].rearrange("p j (c i) -> p c j i", i=LINE),
             )
             return grouped[:].rearrange("p c j -> p (c j)")
 
@@ -90,40 +94,32 @@ def tile_picked_zdin_tanh_po_kernel(
             nc.vector.quantize_mx(out=words[:].bitcast(FP8X4), scales=scales[:], in_=values)
             return words, scales
 
-        def product(out, weights, cols, moving):
+        def product(out, weights, first, moving):
             nc.tensor.matmul_mx(
                 out=out,
-                lhsT=weights[0][:, cols].bitcast(FP8X4),
-                lhsT_scale=weights[1][:, cols],
+                lhsT=weights[0][:, first : first + P].bitcast(FP8X4),
+                lhsT_scale=weights[1][:, first : first + P],
                 rhs=moving[0][:].bitcast(FP8X4),
                 rhs_scale=moving[1][:],
                 start=True,
                 stop=True,
             )
 
-        def product_rows(weights, a, moving, bank, name):
+        def feature_rows(weights, first, moving, bank, name):
             rows = psum.tile([P, moving[0].shape[1]], F32, name=name + "_ps", tag="bank%d" % bank)
-            product(rows[:], weights, slice(a * P, (a + 1) * P), moving)
-            return rows
-
-        def to_sbuf(rows, name):
+            product(rows[:], weights, first, moving)
             held = keep.tile(rows.shape, F32, name=name, align_bytes=64)
             nc.scalar.copy(held[:], rows[:])
             return held
+
+        def places(d, v0, n):
+            return pos_sb[d][:, v0 // 16 : (v0 + n) // 16]
 
         def scores(e, y, name):
             pre = keep.tile([P, D, V], F32, name=name)
             for d in range(D):
                 nc.vector.tensor_tensor(pre[:, d, :], e[:].indirect(pos_sb[d][:]), y[:], MULT)
             return pre
-
-        def fetch(h, v0, n, name):
-            got = keep.tile([P, D, n], F32, name=name, align_bytes=64)
-            for d in range(D):
-                nc.scalar.activation(
-                    got[:, d, :], h[:].indirect(pos_sb[d][:, v0 // 16 : (v0 + n) // 16]), COPY
-                )
-            return got
 
         def squash(pre, name):
             att = keep.tile([P, D, V], F32, name=name)
@@ -133,12 +129,7 @@ def tile_picked_zdin_tanh_po_kernel(
         def weigh(h, att, v0, n, name):
             terms = keep.tile([P, D, n], F32, name=name)
             for d in range(D):
-                nc.vector.tensor_tensor(
-                    terms[:, d, :],
-                    h[:].indirect(pos_sb[d][:, v0 // 16 : (v0 + n) // 16]),
-                    att[:, d, v0 : v0 + n],
-                    MULT,
-                )
+                nc.vector.tensor_tensor(terms[:, d, :], h[:].indirect(places(d, v0, n)), att[:, d, v0 : v0 + n], MULT)
             return terms
 
         def add_turned(terms, c0, out):
@@ -153,82 +144,91 @@ def tile_picked_zdin_tanh_po_kernel(
                 )
 
         def round_z(g, t0, turned):
+            p0 = t0 * P // PACK
             nc.scalar.copy(
-                z_bf[g][:, :, 32 * t0 : 32 * t0 + turned.shape[1] // PACK, :],
+                z_bf[g][:, :, p0 : p0 + turned.shape[1] // PACK, :],
                 turned[:].rearrange("v (p u e) -> v u p e", u=2, e=2),
             )
 
         hist_scales = pick(xs, offs_sb, S, U8, "hist_scales")
         tgt_scales = pick(xs, tgt_sb, V, U8, "tgt_scales")
         hist = pick(xw, offs_sb, S, U32, "hist_words"), hist_scales
-        w2a = quantize(round_weight(("w2", 0), "scalar"), "w2a")
-        w1a = quantize(round_weight(("w1", 0), "scalar"), "w1a")
+        w2_q0 = quantize(round_weight("w2", 0, "scalar"), "w2_q0")
+        w1_q0 = quantize(round_weight("w1", 0, "scalar"), "w1_q0")
         targets = pick(xw, tgt_sb, V, U32, "tgt_words", "w2_bf0"), tgt_scales
-        bf3 = round_weight(("w3", 0), "scalar")
-        e0 = to_sbuf(product_rows(w2a, 0, hist, 0, "e0"), "e0")
-        y0 = to_sbuf(product_rows(w1a, 0, targets, 1, "y0"), "y0")
-        w3a = quantize(bf3, "w3a")
-        bf2 = round_weight(("w2", 1), "vector", "w1_bf0")
-        bf1 = round_weight(("w1", 1), "vector")
-        w2b = quantize(bf2, "w2b")
-        w1b = quantize(bf1, "w1b")
+        w3_bf0 = round_weight("w3", 0, "scalar")
+        e0 = feature_rows(w2_q0, 0, hist, 0, "e0")
+        y0 = feature_rows(w1_q0, 0, targets, 1, "y0")
+        w3_q0 = quantize(w3_bf0, "w3_q0")
+        w2_bf1 = round_weight("w2", 1, "vector", "w1_bf0")
+        w1_bf1 = round_weight("w1", 1, "vector")
+        w2_q1 = quantize(w2_bf1, "w2_q1")
+        w1_q1 = quantize(w1_bf1, "w1_q1")
+
         s0 = scores(e0, y0, "s0")
-        bf3 = round_weight(("w3", 1), "scalar")
-        h0 = to_sbuf(product_rows(w3a, 0, hist, 2, "h0"), "h0")
-        w3b = quantize(bf3, "w3b")
-        e1 = to_sbuf(product_rows(w2b, 0, hist, 3, "e1"), "e1")
-        y1 = to_sbuf(product_rows(w1b, 0, targets, 4, "y1"), "y1")
+        w3_bf1 = round_weight("w3", 1, "scalar")
+        h0 = feature_rows(w3_q0, 0, hist, 2, "h0")
+        w3_q1 = quantize(w3_bf1, "w3_q1")
+        e1 = feature_rows(w2_q1, 0, hist, 3, "e1")
+        y1 = feature_rows(w1_q1, 0, targets, 4, "y1")
         s1 = scores(e1, y1, "s1")
-        w2c = quantize(round_weight(("w2", 2), "vector"), "w2c")
+        w2_q2 = quantize(round_weight("w2", 2, "vector"), "w2_q2")
         a0 = squash(s0, "a0")
         terms0 = weigh(h0, a0, 0, V, "terms0")
-        w1c = quantize(round_weight(("w1", 2), "scalar"), "w1c")
+        w1_q2 = quantize(round_weight("w1", 2, "scalar"), "w1_q2")
         a1 = squash(s1, "a1")
-        h1 = to_sbuf(product_rows(w3b, 0, hist, 5, "h1"), "h1")
+        h1 = feature_rows(w3_q1, 0, hist, 5, "h1")
         terms1 = weigh(h1, a1, 0, V, "terms1")
-        w3c = quantize(round_weight(("w3", 2), "scalar"), "w3c")
-        e2 = to_sbuf(product_rows(w2c, 0, hist, 6, "e2"), "e2")
-        y2 = to_sbuf(product_rows(w1c, 0, targets, 7, "y2"), "y2")
+        w3_q2 = quantize(round_weight("w3", 2, "scalar"), "w3_q2")
+        e2 = feature_rows(w2_q2, 0, hist, 6, "e2")
+        y2 = feature_rows(w1_q2, 0, targets, 7, "y2")
         s2 = scores(e2, y2, "s2")
-        e3 = to_sbuf(product_rows(w2c, 1, hist, 0, "e3"), "e3")
-        y3 = to_sbuf(product_rows(w1c, 1, targets, 1, "y3"), "y3")
+        e3 = feature_rows(w2_q2, P, hist, 0, "e3")
+        y3 = feature_rows(w1_q2, P, targets, 1, "y3")
         s3 = scores(e3, y3, "s3")
-        h2 = to_sbuf(product_rows(w3c, 0, hist, 2, "h2"), "h2")
-        h3 = to_sbuf(product_rows(w3c, 1, hist, 3, "h3"), "h3")
+        h2 = feature_rows(w3_q2, 0, hist, 2, "h2")
+        h3 = feature_rows(w3_q2, P, hist, 3, "h3")
         a2 = squash(s2, "a2")
         terms2 = weigh(h2, a2, 0, V, "terms2")
         a3 = squash(s3, "a3")
-        values3 = fetch(h3, P, P, "values3")
-        last = [weigh(h3, a3, 0, P, "terms3_0"), keep.tile([P, D, P], F32, name="terms3_1")]
-        nc.vector.tensor_tensor(last[1][:], values3[:], a3[:, :, P:], MULT)
 
-        z_t = [psum.tile([P, 3 * P], F32, name="z_t%d" % g, tag="bank%d" % (2 + g)) for g in range(2)]
-        z_bf = [keep.tile([P, 2, P, 2], BF16, name="z_bf%d" % g) for g in range(2)]
+        values3 = keep.tile([P, D, P], F32, name="values3", align_bytes=64)
+        for d in range(D):
+            nc.scalar.activation(values3[:, d, :], h3[:].indirect(places(d, P, P)), COPY)
+        terms3 = [weigh(h3, a3, 0, P, "terms3_0"), keep.tile([P, D, P], F32, name="terms3_1")]
+        nc.vector.tensor_tensor(terms3[1][:], values3[:], a3[:, :, P:], MULT)
+
+        z_early = [psum.tile([P, 3 * P], F32, name="z_early%d" % g, tag="bank%d" % (2 + g)) for g in range(GROUPS)]
+        z_bf = [keep.tile([P, 2, P, 2], BF16, name="z_bf%d" % g) for g in range(GROUPS)]
         for t, terms in enumerate((terms0, terms1, terms2)):
-            for g in range(2):
-                add_turned(terms, g * P, z_t[g][:, t * P : (t + 1) * P])
-        for g in range(2):
-            round_z(g, 0, z_t[g])
+            for g in range(GROUPS):
+                add_turned(terms, g * P, z_early[g][:, t * P : (t + 1) * P])
+        for g in range(GROUPS):
+            round_z(g, 0, z_early[g])
+
         w4_bf = []
-        for half in range(2):
-            dealt = keep.tile([P, 2, P, PACK], BF16, name="w4_bf%d" % half, align_bytes=64, tag=("h3", "values3")[half])
+        for half, tag in enumerate(("h3", "values3")):
+            dealt = keep.tile([P, 2, P, PACK], BF16, name="w4_bf%d" % half, align_bytes=64, tag=tag)
             nc.vector.tensor_copy(
-                dealt[:].rearrange("p t m j -> p m j t"),
-                w4_raw[:].rearrange("p j (m t) -> p m j t", t=PACK)[:, :, :, 2 * half : 2 * half + 2],
+                dealt[:].rearrange("p r m j -> p m j r"),
+                w4_raw[:].rearrange("p j (m r) -> p m j r", r=PACK)[:, :, :, 2 * half : 2 * half + 2],
             )
             w4_bf.append(dealt)
-        w4q = [quantize(w4_bf[half][:].rearrange("p t m j -> p (t m j)"), "w4q%d" % half) for half in range(2)]
+        w4_q = [
+            quantize(dealt[:].rearrange("p r m j -> p (r m j)"), "w4_q%d" % half) for half, dealt in enumerate(w4_bf)
+        ]
 
         out_words = keep.tile([P, V], U32, name="out_words", align_bytes=64)
         out_scales = keep.tile([P, V], U8, name="out_scales", align_bytes=64)
-        out_rows = out_0.rearrange("(p t) v -> p t v", t=PACK)
+        out_rows = out_0.rearrange("(p r) v -> p r v", r=PACK)
         word_rows = out_1[0].rearrange("p c r -> p (c r)").bitcast(I32)
-        zq = []
-        for g in range(2):
+
+        for g in range(GROUPS):
             z_last = psum.tile([P, P], F32, name="z_last%d" % g, tag="bank%d" % g)
-            add_turned(last[g], 0, z_last[:])
+            add_turned(terms3[g], 0, z_last[:])
             round_z(g, 3, z_last)
-        for g in range(2):
+        z_q = []
+        for g in range(GROUPS):
             back = psum.tile([P, 2, P], F32, name="back%d" % g, tag="bank%d" % (4 + g))
             pairs = z_bf[g][:].rearrange("v u p e -> v (u p e)").bitcast(F32)
             for u in range(2):
@@ -237,26 +237,29 @@ def tile_picked_zdin_tanh_po_kernel(
             nc.scalar.copy(
                 z_k[:].bitcast(F32).rearrange("p (v u) -> p v u", u=2), back[:].rearrange("p u v -> p v u")
             )
-            zq.append(quantize(z_k[:], "zq%d" % g))
-        for g in range(2):
+            z_q.append(quantize(z_k[:], "z_q%d" % g))
+
+        for g, first_bank in enumerate((6, 2)):
             cols = slice(g * P, (g + 1) * P)
-            res = psum.tile([P, PACK, P], F32, name="res%d" % g, tag="bank%d" % (6 + g))
-            for t in range(PACK):
-                product(res[:, t, :], w4q[t // 2], slice(t % 2 * P, (t % 2 + 1) * P), zq[g])
             res_sb = keep.tile([P, PACK, P], F32, name="res_sb%d" % g)
-            nc.scalar.copy(res_sb[:], res[:])
+            for half, engine in enumerate(("scalar", "vector")):
+                res = psum.tile([P, 2, P], F32, name="res%d_%d" % (g, half), tag="bank%d" % (first_bank + half))
+                for r in range(2):
+                    product(res[:, r, :], w4_q[half], r * P, z_q[g])
+                copy_on(engine, res_sb[:, 2 * half : 2 * half + 2, :], res[:])
             nc.sync.dma_start(out_rows[:, :, cols], res_sb[:])
             res_bf = keep.tile([P, P, PACK], BF16, name="res_bf%d" % g, align_bytes=64)
             nc.vector.tensor_copy(
-                res_bf[:].rearrange("p (c i) t -> p c t i", i=4), res_sb[:].rearrange("p t (c i) -> p c t i", i=4)
+                res_bf[:].rearrange("p (c i) r -> p c r i", i=LINE),
+                res_sb[:].rearrange("p r (c i) -> p c r i", i=LINE),
             )
             nc.vector.quantize_mx(
                 out=out_words[:, cols].bitcast(FP8X4),
                 scales=out_scales[:, cols],
-                in_=res_bf[:].rearrange("p c t -> p (c t)"),
+                in_=res_bf[:].rearrange("p c r -> p (c r)"),
             )
             nc.sync.dma_start(word_rows[:, cols], out_words[:, cols].bitcast(I32))
-        for q in range(4):
+        for q in range(QUADRANTS):
             queue = nc.scalar if q % 2 else nc.sync
             queue.dma_start(
                 out_2[0, 4 * q : 4 * q + 4, :].bitcast(I32), out_scales[32 * q : 32 * q + 4, :].bitcast(I32)

from contextlib import ExitStack

import concourse.mybir as mybir
from concourse.masks import make_identity

F32 = mybir.dt.float32
BF16 = mybir.dt.bfloat16
I32 = mybir.dt.int32
U32 = mybir.dt.uint32
U16 = mybir.dt.uint16
U8 = mybir.dt.uint8
FP8X4 = mybir.dt.float8_e4m3fn_x4
MULT = mybir.AluOpType.mult
COPY = mybir.ActivationFunctionType.Copy
TANH = mybir.ActivationFunctionType.Tanh

P = 128
PACK = 4
QUADRANTS = 4
GROUPS = 2
LINE = 4
K, T, S, V, H, N = 512, 1024, 512, 256, 512, 512
D = 3
PIECES = ((0, P), (P, P), (2 * P, 2 * P))
FLOPS = 2 * K * (N * S + H * S + N * V) + 2 * H * N * V


def tile_picked_zdin_tanh_po_kernel(
    tc, x_words, x_scales, w1, w2, w3, w4, offs, tgt, pos1, pos2, pos3, out_0, out_1, out_2
):
    nc = tc.nc
    with ExitStack() as ctx:
        keep = ctx.enter_context(tc.tile_pool(name="keep", bufs=1))
        psum = ctx.enter_context(tc.psum_pool(name="psum", bufs=1))

        def load_list(src, name):
            lst = keep.tile([P, src.shape[1]], U16, name=name)
            nc.sync.dma_start(lst[:], src)
            return lst

        def load_weight(w, c0, width, name):
            raw = keep.tile([P, PACK, width], F32, name=name)
            nc.sync.dma_start(raw[:], w[:, c0 : c0 + width].rearrange("(p j) c -> p j c", j=PACK))
            return raw

        xs = keep.tile([P, T], U8, name="xs")
        nc.gpsimd.memset(xs[:].bitcast(U32), 0)
        for q in range(QUADRANTS):
            queue = nc.scalar if q % 2 else nc.sync
            queue.dma_start(
                xs[32 * q : 32 * q + 4, :].bitcast(I32), x_scales[0, 4 * q : 4 * q + 4, :].bitcast(I32)
            )
        offs_sb = load_list(offs, "offs_sb")
        xw = keep.tile([P, T], U32, name="xw")
        nc.scalar.dma_start(xw[:].bitcast(I32), x_words[0].rearrange("p c r -> p (c r)").bitcast(I32))
        tgt_sb = load_list(tgt, "tgt_sb")
        raws = {}
        for piece, (c0, width) in enumerate(PIECES):
            for name, w in (("w2", w2), ("w1", w1), ("w3", w3)):
                raws[name, piece] = load_weight(w, c0, width, "%s_raw%d" % (name, piece))
            if piece == 0:
                pos_sb = [load_list(src, "pos_sb%d" % d) for d, src in enumerate((pos1, pos2, pos3))]
        w4_raw = load_weight(w4, 0, N, "w4_raw")

        ident = keep.tile([P, P], F32, name="ident")
        make_identity(nc, ident[:])

        def copy_on(engine, out, in_):
            if engine == "vector":
                nc.vector.tensor_copy(out, in_)
            else:
                nc.scalar.copy(out, in_)

        def pick(table, lst, n, dtype, name, tag=""):
            picked = keep.tile([P, n], dtype, name=name, tag=tag or name, align_bytes=64)
            nc.vector.tensor_copy(picked[:], table[:].indirect(lst[:]))
            return picked

        def round_weight(name, piece, engine, tag=""):
            raw = raws[name, piece]
            tile_name = "%s_bf%d" % (name, piece)
            grouped = keep.tile([P, raw.shape[2], PACK], BF16, name=tile_name, tag=tag or tile_name, align_bytes=64)
            copy_on(
                engine,
                grouped[:].rearrange("p (c i) j -> p c j i", i=LINE),
                raw[:].rearrange("p j (c i) -> p c j i", i=LINE),
            )
            return grouped[:].rearrange("p c j -> p (c j)")

        def quantize(values, name):
            n = values.shape[1] // PACK
            words = keep.tile([P, n], U32, name=name + "_words", align_bytes=64)
            scales = keep.tile([P, n], U8, name=name + "_scales", align_bytes=64)
            nc.vector.quantize_mx(out=words[:].bitcast(FP8X4), scales=scales[:], in_=values)
            return words, scales

        def product(out, weights, first, moving):
            nc.tensor.matmul_mx(
                out=out,
                lhsT=weights[0][:, first : first + P].bitcast(FP8X4),
                lhsT_scale=weights[1][:, first : first + P],
                rhs=moving[0][:].bitcast(FP8X4),
                rhs_scale=moving[1][:],
                start=True,
                stop=True,
            )

        def feature_rows(weights, first, moving, bank, name):
            rows = psum.tile([P, moving[0].shape[1]], F32, name=name + "_ps", tag="bank%d" % bank)
            product(rows[:], weights, first, moving)
            held = keep.tile(rows.shape, F32, name=name, align_bytes=64)
            nc.scalar.copy(held[:], rows[:])
            return held

        def places(d, v0, n):
            return pos_sb[d][:, v0 // 16 : (v0 + n) // 16]

        def scores(e, y, name):
            pre = keep.tile([P, D, V], F32, name=name)
            for d in range(D):
                nc.vector.tensor_tensor(pre[:, d, :], e[:].indirect(pos_sb[d][:]), y[:], MULT)
            return pre

        def squash(pre, name):
            att = keep.tile([P, D, V], F32, name=name)
            nc.scalar.activation(att[:].rearrange("p d v -> p (d v)"), pre[:].rearrange("p d v -> p (d v)"), TANH)
            return att

        def weigh(h, att, v0, n, name):
            terms = keep.tile([P, D, n], F32, name=name)
            for d in range(D):
                nc.vector.tensor_tensor(terms[:, d, :], h[:].indirect(places(d, v0, n)), att[:, d, v0 : v0 + n], MULT)
            return terms

        def add_turned(terms, c0, out):
            for d in range(D):
                nc.tensor.matmul(
                    out,
                    lhsT=terms[:, d, c0 : c0 + P],
                    rhs=ident[:],
                    is_transpose=True,
                    start=(d == 0),
                    stop=(d == D - 1),
                )

        def round_z(g, t0, turned):
            p0 = t0 * P // PACK
            nc.scalar.copy(
                z_bf[g][:, :, p0 : p0 + turned.shape[1] // PACK, :],
                turned[:].rearrange("v (p u e) -> v u p e", u=2, e=2),
            )

        hist_scales = pick(xs, offs_sb, S, U8, "hist_scales")
        tgt_scales = pick(xs, tgt_sb, V, U8, "tgt_scales")
        hist = pick(xw, offs_sb, S, U32, "hist_words"), hist_scales
        w2_q0 = quantize(round_weight("w2", 0, "scalar"), "w2_q0")
        w1_q0 = quantize(round_weight("w1", 0, "scalar"), "w1_q0")
        targets = pick(xw, tgt_sb, V, U32, "tgt_words", "w2_bf0"), tgt_scales
        w3_bf0 = round_weight("w3", 0, "scalar")
        e0 = feature_rows(w2_q0, 0, hist, 0, "e0")
        y0 = feature_rows(w1_q0, 0, targets, 1, "y0")
        w3_q0 = quantize(w3_bf0, "w3_q0")
        w2_bf1 = round_weight("w2", 1, "vector", "w1_bf0")
        w1_bf1 = round_weight("w1", 1, "vector")
        w2_q1 = quantize(w2_bf1, "w2_q1")
        w1_q1 = quantize(w1_bf1, "w1_q1")

        s0 = scores(e0, y0, "s0")
        w3_bf1 = round_weight("w3", 1, "scalar")
        h0 = feature_rows(w3_q0, 0, hist, 2, "h0")
        w3_q1 = quantize(w3_bf1, "w3_q1")
        e1 = feature_rows(w2_q1, 0, hist, 3, "e1")
        y1 = feature_rows(w1_q1, 0, targets, 4, "y1")
        s1 = scores(e1, y1, "s1")
        w2_q2 = quantize(round_weight("w2", 2, "vector"), "w2_q2")
        a0 = squash(s0, "a0")
        terms0 = weigh(h0, a0, 0, V, "terms0")
        w1_q2 = quantize(round_weight("w1", 2, "scalar"), "w1_q2")
        a1 = squash(s1, "a1")
        h1 = feature_rows(w3_q1, 0, hist, 5, "h1")
        terms1 = weigh(h1, a1, 0, V, "terms1")
        w3_q2 = quantize(round_weight("w3", 2, "scalar"), "w3_q2")
        e2 = feature_rows(w2_q2, 0, hist, 6, "e2")
        y2 = feature_rows(w1_q2, 0, targets, 7, "y2")
        s2 = scores(e2, y2, "s2")
        e3 = feature_rows(w2_q2, P, hist, 0, "e3")
        y3 = feature_rows(w1_q2, P, targets, 1, "y3")
        s3 = scores(e3, y3, "s3")
        h2 = feature_rows(w3_q2, 0, hist, 2, "h2")
        h3 = feature_rows(w3_q2, P, hist, 3, "h3")
        a2 = squash(s2, "a2")
        terms2 = weigh(h2, a2, 0, V, "terms2")
        a3 = squash(s3, "a3")

        values3 = keep.tile([P, D, P], F32, name="values3", align_bytes=64)
        for d in range(D):
            nc.scalar.activation(values3[:, d, :], h3[:].indirect(places(d, P, P)), COPY)
        terms3 = [weigh(h3, a3, 0, P, "terms3_0"), keep.tile([P, D, P], F32, name="terms3_1")]
        nc.vector.tensor_tensor(terms3[1][:], values3[:], a3[:, :, P:], MULT)

        z_early = [psum.tile([P, 3 * P], F32, name="z_early%d" % g, tag="bank%d" % (2 + g)) for g in range(GROUPS)]
        z_bf = [keep.tile([P, 2, P, 2], BF16, name="z_bf%d" % g) for g in range(GROUPS)]
        for t, terms in enumerate((terms0, terms1, terms2)):
            for g in range(GROUPS):
                add_turned(terms, g * P, z_early[g][:, t * P : (t + 1) * P])
        for g in range(GROUPS):
            round_z(g, 0, z_early[g])

        w4_bf = []
        for half, tag in enumerate(("h3", "values3")):
            dealt = keep.tile([P, 2, P, PACK], BF16, name="w4_bf%d" % half, align_bytes=64, tag=tag)
            nc.vector.tensor_copy(
                dealt[:].rearrange("p r m j -> p m j r"),
                w4_raw[:].rearrange("p j (m r) -> p m j r", r=PACK)[:, :, :, 2 * half : 2 * half + 2],
            )
            w4_bf.append(dealt)
        w4_q = [
            quantize(dealt[:].rearrange("p r m j -> p (r m j)"), "w4_q%d" % half) for half, dealt in enumerate(w4_bf)
        ]

        out_words = keep.tile([P, V], U32, name="out_words", align_bytes=64)
        out_scales = keep.tile([P, V], U8, name="out_scales", align_bytes=64)
        out_rows = out_0.rearrange("(p r) v -> p r v", r=PACK)
        word_rows = out_1[0].rearrange("p c r -> p (c r)").bitcast(I32)

        for g in range(GROUPS):
            z_last = psum.tile([P, P], F32, name="z_last%d" % g, tag="bank%d" % g)
            add_turned(terms3[g], 0, z_last[:])
            round_z(g, 3, z_last)
        z_q = []
        for g in range(GROUPS):
            back = psum.tile([P, 2, P], F32, name="back%d" % g, tag="bank%d" % (4 + g))
            pairs = z_bf[g][:].rearrange("v u p e -> v (u p e)").bitcast(F32)
            for u in range(2):
                nc.tensor.transpose(back[:, u, :], pairs[:, u * P : (u + 1) * P], ident[:])
            z_k = keep.tile([P, P * PACK], BF16, name="z_k%d" % g, align_bytes=64)
            nc.scalar.copy(
                z_k[:].bitcast(F32).rearrange("p (v u) -> p v u", u=2), back[:].rearrange("p u v -> p v u")
            )
            z_q.append(quantize(z_k[:], "z_q%d" % g))

        for g, first_bank in enumerate((6, 2)):
            cols = slice(g * P, (g + 1) * P)
            res_sb = keep.tile([P, PACK, P], F32, name="res_sb%d" % g)
            for half, engine in enumerate(("scalar", "vector")):
                res = psum.tile([P, 2, P], F32, name="res%d_%d" % (g, half), tag="bank%d" % (first_bank + half))
                for r in range(2):
                    product(res[:, r, :], w4_q[half], r * P, z_q[g])
                copy_on(engine, res_sb[:, 2 * half : 2 * half + 2, :], res[:])
            nc.sync.dma_start(out_rows[:, :, cols], res_sb[:])
            res_bf = keep.tile([P, P, PACK], BF16, name="res_bf%d" % g, align_bytes=64)
            nc.vector.tensor_copy(
                res_bf[:].rearrange("p (c i) r -> p c r i", i=LINE),
                res_sb[:].rearrange("p r (c i) -> p c r i", i=LINE),
            )
            nc.vector.quantize_mx(
                out=out_words[:, cols].bitcast(FP8X4),
                scales=out_scales[:, cols],
                in_=res_bf[:].rearrange("p c r -> p (c r)"),
            )
            nc.sync.dma_start(word_rows[:, cols], out_words[:, cols].bitcast(I32))
        for q in range(QUADRANTS):
            queue = nc.scalar if q % 2 else nc.sync
            queue.dma_start(
                out_2[0, 4 * q : 4 * q + 4, :].bitcast(I32), out_scales[32 * q : 32 * q + 4, :].bitcast(I32)
            )
